import numpy as np
import ml_dtypes

BF16 = ml_dtypes.bfloat16


def bf(x):
    return np.asarray(x, np.float32).astype(BF16)


def f32(x):
    return np.asarray(x, np.float32)


def f64(x):
    return np.asarray(x).astype(np.float64)


def striped(idx):
    return np.tile(idx.reshape(-1, 16).T, (8, 1))


S, K, M, N, B, Q = 512, 256, 128, 256, 4, 64


def setup_inputs():
    return {"base": bf(np.random.standard_normal((B, M, S))), "x": bf(np.random.standard_normal((K, N))), "w": bf(np.random.standard_normal((K, M)) / np.sqrt(K)), "c": f32(0.2 + 0.8 * np.random.random_sample((1, S))), "offs": striped(np.random.permutation(S)[:N])}


def reference(base, x, w, c, offs):
    idx = offs[:16].T.reshape(-1)
    z = f64(base).copy()
    for i in range(B):
        z[i][:, idx[i * Q : (i + 1) * Q]] += f64(w).T @ f64(x)[:, i * Q : (i + 1) * Q]
    return z * f64(c)

@@ -1,0 +1,53 @@
+import concourse.mybir as mybir
+from concourse.masks import make_identity
+
+P = 128
+SEQS = 4
+TOKENS = 512
+PIECE = 64
+K_BLOCKS = 2
+COLS = PIECE // 16
+FLOPS = 2 * (P * K_BLOCKS) * P * (SEQS * PIECE)
+
+BF16, F32, U16 = mybir.dt.bfloat16, mybir.dt.float32, mybir.dt.uint16
+
+
+def tile_scatter_matmul_kernel(tc, base, x, w, c, offs, out):
+    nc = tc.nc
+    with (
+        tc.tile_pool(name="held", bufs=1) as held,
+        tc.psum_pool(name="psum", bufs=1) as psum,
+    ):
+        base_t = held.tile([P, SEQS, TOKENS], BF16)
+        nc.sync.dma_start(base_t[:], base.rearrange("i m t -> m i t"))
+        w_t = held.tile([P, K_BLOCKS, P], BF16)
+        nc.sync.dma_start(w_t[:], w.rearrange("(p a) m -> p a m", a=K_BLOCKS))
+        x_t = held.tile([P, K_BLOCKS, SEQS * PIECE], BF16)
+        nc.sync.dma_start(x_t[:], x.rearrange("(p a) j -> p a j", a=K_BLOCKS))
+        offsets = held.tile([P, SEQS * COLS], U16)
+        nc.sync.dma_start(offsets[:], offs)
+        c_t = held.tile([P, TOKENS], F32)
+        nc.sync.dma_start(c_t[:], c.rearrange("o t -> (o t)").partition_broadcast(P))
+
+        ident = held.tile([P, P], BF16)
+        make_identity(nc, ident[:])
+
+        windows = [psum.tile([P, TOKENS], F32, name=f"window{i}") for i in range(SEQS)]
+        for i in range(SEQS):
+            nc.tensor.matmul(windows[i][:], ident[:], base_t[:, i, :], start=True, stop=False)
+
+        for i in range(SEQS):
+            places = windows[i][:].indirect(offsets[:, i * COLS : (i + 1) * COLS])
+            for a in range(K_BLOCKS):
+                nc.tensor.matmul(
+                    places,
+                    w_t[:, a, :],
+                    x_t[:, a, i * PIECE : (i + 1) * PIECE],
+                    start=False,
+                    stop=(a == K_BLOCKS - 1),
+                )
+
+        for i in range(SEQS):
+            z = held.tile([P, TOKENS], F32, name=f"z{i}")
+            nc.vector.tensor_tensor(z[:], windows[i][:], c_t[:], mybir.AluOpType.mult)
+            nc.sync.dma_start(out[i], z[:])

@@ -7,6 +7,7 @@ TOKENS = 512
 PIECE = 64
 K_BLOCKS = 2
 COLS = PIECE // 16
+WARM_UPS = 6
 FLOPS = 2 * (P * K_BLOCKS) * P * (SEQS * PIECE)
 
 BF16, F32, U16 = mybir.dt.bfloat16, mybir.dt.float32, mybir.dt.uint16
@@ -28,6 +29,12 @@ def tile_scatter_matmul_kernel(tc, base, x, w, c, offs, out):
         nc.sync.dma_start(offsets[:], offs)
         c_t = held.tile([P, TOKENS], F32)
         nc.sync.dma_start(c_t[:], c.rearrange("o t -> (o t)").partition_broadcast(P))
+
+        zeros = held.tile([P, TOKENS], BF16)
+        nc.vector.memset(zeros[:], 0.0)
+        spare = psum.tile([P, TOKENS], F32)
+        for n in range(WARM_UPS):
+            nc.tensor.matmul(spare[:], zeros[:, :P], zeros[:], start=True, stop=True)
 
         ident = held.tile([P, P], BF16)
         make_identity(nc, ident[:])

@@ -19,16 +19,19 @@ def tile_scatter_matmul_kernel(tc, base, x, w, c, offs, out):
         tc.tile_pool(name="held", bufs=1) as held,
         tc.psum_pool(name="psum", bufs=1) as psum,
     ):
-        base_t = held.tile([P, SEQS, TOKENS], BF16)
-        nc.sync.dma_start(base_t[:], base.rearrange("i m t -> m i t"))
+        halves = []
+        for h in range(2):
+            half = held.tile([P, SEQS // 2, TOKENS], BF16, name=f"base_half{h}")
+            nc.sync.dma_start(half[:], base[2 * h : 2 * h + 2].rearrange("i m t -> m i t"))
+            halves.append(half)
         w_t = held.tile([P, K_BLOCKS, P], BF16)
-        nc.sync.dma_start(w_t[:], w.rearrange("(p a) m -> p a m", a=K_BLOCKS))
+        nc.scalar.dma_start(w_t[:], w.rearrange("(p a) m -> p a m", a=K_BLOCKS))
         x_t = held.tile([P, K_BLOCKS, SEQS * PIECE], BF16)
-        nc.sync.dma_start(x_t[:], x.rearrange("(p a) j -> p a j", a=K_BLOCKS))
+        nc.scalar.dma_start(x_t[:], x.rearrange("(p a) j -> p a j", a=K_BLOCKS))
         offsets = held.tile([P, SEQS * COLS], U16)
         nc.sync.dma_start(offsets[:], offs)
         c_t = held.tile([P, TOKENS], F32)
-        nc.sync.dma_start(c_t[:], c.rearrange("o t -> (o t)").partition_broadcast(P))
+        nc.scalar.dma_start(c_t[:], c.rearrange("o t -> (o t)").partition_broadcast(P))
 
         zeros = held.tile([P, TOKENS], BF16)
         nc.vector.memset(zeros[:], 0.0)
@@ -41,7 +44,7 @@ def tile_scatter_matmul_kernel(tc, base, x, w, c, offs, out):
 
         windows = [psum.tile([P, TOKENS], F32, name=f"window{i}") for i in range(SEQS)]
         for i in range(SEQS):
-            nc.tensor.matmul(windows[i][:], ident[:], base_t[:, i, :], start=True, stop=False)
+            nc.tensor.matmul(windows[i][:], ident[:], halves[i // 2][:, i % 2, :], start=True, stop=False)
 
         for i in range(SEQS):
             places = windows[i][:].indirect(offsets[:, i * COLS : (i + 1) * COLS])

@@ -7,7 +7,7 @@ TOKENS = 512
 PIECE = 64
 K_BLOCKS = 2
 COLS = PIECE // 16
-WARM_UPS = 6
+WARM_UPS = 2
 FLOPS = 2 * (P * K_BLOCKS) * P * (SEQS * PIECE)
 
 BF16, F32, U16 = mybir.dt.bfloat16, mybir.dt.float32, mybir.dt.uint16
@@ -19,6 +19,9 @@ def tile_scatter_matmul_kernel(tc, base, x, w, c, offs, out):
         tc.tile_pool(name="held", bufs=1) as held,
         tc.psum_pool(name="psum", bufs=1) as psum,
     ):
+        c_row = held.tile([1, TOKENS], F32)
+        nc.scalar.dma_start(c_row[:], c)
+
         halves = []
         for h in range(2):
             half = held.tile([P, SEQS // 2, TOKENS], BF16, name=f"base_half{h}")
@@ -30,14 +33,19 @@ def tile_scatter_matmul_kernel(tc, base, x, w, c, offs, out):
         nc.scalar.dma_start(x_t[:], x.rearrange("(p a) j -> p a j", a=K_BLOCKS))
         offsets = held.tile([P, SEQS * COLS], U16)
         nc.sync.dma_start(offsets[:], offs)
-        c_t = held.tile([P, TOKENS], F32)
-        nc.scalar.dma_start(c_t[:], c.rearrange("o t -> (o t)").partition_broadcast(P))
 
         zeros = held.tile([P, TOKENS], BF16)
         nc.vector.memset(zeros[:], 0.0)
         spare = psum.tile([P, TOKENS], F32)
         for n in range(WARM_UPS):
             nc.tensor.matmul(spare[:], zeros[:, :P], zeros[:], start=True, stop=True)
+
+        ones = held.tile([1, P], F32)
+        nc.vector.memset(ones[:], 1.0)
+        c_bank = psum.tile([P, TOKENS], F32)
+        nc.tensor.matmul(c_bank[:], ones[:], c_row[:], start=True, stop=True)
+        c_t = held.tile([P, TOKENS], F32)
+        nc.vector.tensor_copy(c_t[:], c_bank[:])
 
         ident = held.tile([P, P], BF16)
         make_identity(nc, ident[:])

@@ -7,7 +7,7 @@ TOKENS = 512
 PIECE = 64
 K_BLOCKS = 2
 COLS = PIECE // 16
-WARM_UPS = 2
+WARM_UPS = 4
 FLOPS = 2 * (P * K_BLOCKS) * P * (SEQS * PIECE)
 
 BF16, F32, U16 = mybir.dt.bfloat16, mybir.dt.float32, mybir.dt.uint16
@@ -19,14 +19,15 @@ def tile_scatter_matmul_kernel(tc, base, x, w, c, offs, out):
         tc.tile_pool(name="held", bufs=1) as held,
         tc.psum_pool(name="psum", bufs=1) as psum,
     ):
-        c_row = held.tile([1, TOKENS], F32)
-        nc.scalar.dma_start(c_row[:], c)
+        c_row = held.tile([P, TOKENS], F32)
+        nc.gpsimd.memset(c_row[:], 0.0)
 
         halves = []
         for h in range(2):
             half = held.tile([P, SEQS // 2, TOKENS], BF16, name=f"base_half{h}")
             nc.sync.dma_start(half[:], base[2 * h : 2 * h + 2].rearrange("i m t -> m i t"))
             halves.append(half)
+        nc.sync.dma_start(c_row[:1, :], c)
         w_t = held.tile([P, K_BLOCKS, P], BF16)
         nc.scalar.dma_start(w_t[:], w.rearrange("(p a) m -> p a m", a=K_BLOCKS))
         x_t = held.tile([P, K_BLOCKS, SEQS * PIECE], BF16)
@@ -40,19 +41,19 @@ def tile_scatter_matmul_kernel(tc, base, x, w, c, offs, out):
         for n in range(WARM_UPS):
             nc.tensor.matmul(spare[:], zeros[:, :P], zeros[:], start=True, stop=True)
 
-        ones = held.tile([1, P], F32)
-        nc.vector.memset(ones[:], 1.0)
-        c_bank = psum.tile([P, TOKENS], F32)
-        nc.tensor.matmul(c_bank[:], ones[:], c_row[:], start=True, stop=True)
-        c_t = held.tile([P, TOKENS], F32)
-        nc.vector.tensor_copy(c_t[:], c_bank[:])
-
         ident = held.tile([P, P], BF16)
         make_identity(nc, ident[:])
 
         windows = [psum.tile([P, TOKENS], F32, name=f"window{i}") for i in range(SEQS)]
         for i in range(SEQS):
             nc.tensor.matmul(windows[i][:], ident[:], halves[i // 2][:, i % 2, :], start=True, stop=False)
+
+        ones = held.tile([P, P], F32)
+        nc.vector.memset(ones[:], 1.0)
+        c_bank = psum.tile([P, TOKENS], F32)
+        nc.tensor.matmul(c_bank[:], ones[:], c_row[:], start=True, stop=True)
+        c_t = held.tile([P, TOKENS], F32)
+        nc.vector.tensor_copy(c_t[:], c_bank[:])
 
         for i in range(SEQS):
             places = windows[i][:].indirect(offsets[:, i * COLS : (i + 1) * COLS])

import concourse.mybir as mybir
from concourse.masks import make_identity

P = 128
SEQS = 4
TOKENS = 512
PIECE = 64
K_BLOCKS = 2
COLS = PIECE // 16
WARM_UPS = 4
FLOPS = 2 * (P * K_BLOCKS) * P * (SEQS * PIECE)

BF16, F32, U16 = mybir.dt.bfloat16, mybir.dt.float32, mybir.dt.uint16


def tile_scatter_matmul_kernel(tc, base, x, w, c, offs, out):
    nc = tc.nc
    with (
        tc.tile_pool(name="held", bufs=1) as held,
        tc.psum_pool(name="psum", bufs=1) as psum,
    ):
        c_row = held.tile([P, TOKENS], F32)
        nc.gpsimd.memset(c_row[:], 0.0)

        halves = []
        for h in range(2):
            half = held.tile([P, SEQS // 2, TOKENS], BF16, name=f"base_half{h}")
            nc.sync.dma_start(half[:], base[2 * h : 2 * h + 2].rearrange("i m t -> m i t"))
            halves.append(half)
        nc.sync.dma_start(c_row[:1, :], c)
        w_t = held.tile([P, K_BLOCKS, P], BF16)
        nc.scalar.dma_start(w_t[:], w.rearrange("(p a) m -> p a m", a=K_BLOCKS))
        x_t = held.tile([P, K_BLOCKS, SEQS * PIECE], BF16)
        nc.scalar.dma_start(x_t[:], x.rearrange("(p a) j -> p a j", a=K_BLOCKS))
        offsets = held.tile([P, SEQS * COLS], U16)
        nc.sync.dma_start(offsets[:], offs)

        zeros = held.tile([P, TOKENS], BF16)
        nc.vector.memset(zeros[:], 0.0)
        spare = psum.tile([P, TOKENS], F32)
        for n in range(WARM_UPS):
            nc.tensor.matmul(spare[:], zeros[:, :P], zeros[:], start=True, stop=True)

        ident = held.tile([P, P], BF16)
        make_identity(nc, ident[:])

        windows = [psum.tile([P, TOKENS], F32, name=f"window{i}") for i in range(SEQS)]
        for i in range(SEQS):
            nc.tensor.matmul(windows[i][:], ident[:], halves[i // 2][:, i % 2, :], start=True, stop=False)

        ones = held.tile([P, P], F32)
        nc.vector.memset(ones[:], 1.0)
        c_bank = psum.tile([P, TOKENS], F32)
        nc.tensor.matmul(c_bank[:], ones[:], c_row[:], start=True, stop=True)
        c_t = held.tile([P, TOKENS], F32)
        nc.vector.tensor_copy(c_t[:], c_bank[:])

        for i in range(SEQS):
            places = windows[i][:].indirect(offsets[:, i * COLS : (i + 1) * COLS])
            for a in range(K_BLOCKS):
                nc.tensor.matmul(
                    places,
                    w_t[:, a, :],
                    x_t[:, a, i * PIECE : (i + 1) * PIECE],
                    start=False,
                    stop=(a == K_BLOCKS - 1),
                )

        for i in range(SEQS):
            z = held.tile([P, TOKENS], F32, name=f"z{i}")
            nc.vector.tensor_tensor(z[:], windows[i][:], c_t[:], mybir.AluOpType.mult)
            nc.sync.dma_start(out[i], z[:])
